import numpy as np
import ml_dtypes


def mxq(x, axis, fmt="e4m3"):
    dtype, down = {"e4m3": (ml_dtypes.float8_e4m3fn, 7), "e5m2": (ml_dtypes.float8_e5m2, 14)}[fmt]
    v = np.moveaxis(np.asarray(x, np.float32).astype(ml_dtypes.bfloat16).astype(np.float64), axis, -1)
    blocks = v.reshape(v.shape[:-1] + (-1, 32))
    amax = np.abs(blocks).max(-1, keepdims=True)
    byte = np.maximum(np.where(amax > 0, np.frexp(amax)[1] - 1 + 127, 0) - down, 1)
    scale = np.exp2(byte - 127.0)
    codes = (blocks / scale).astype(np.float32).astype(dtype).astype(np.float64)
    return np.moveaxis((codes * scale).reshape(v.shape), -1, axis)


WIDE = False


def mx_kscale(k):
    if not WIDE:
        return np.ones(k)
    levels = np.array([10, -10, 5, -5, 0])
    if k % 512:
        return np.exp2(np.random.permutation(np.resize(levels, k // 32))).repeat(32)
    a = np.empty((k // 512, 16))
    for p in range(k // 512):
        a[p, :8] = np.random.permutation(np.resize(levels, 8))
        for g in range(8):
            far = levels[np.abs(levels - a[p, g]) >= 10]
            a[p, g + 8] = far[np.random.randint(len(far))]
    return np.exp2(a.ravel()).repeat(32)


def f64(x):
    return np.asarray(x).astype(np.float64)


def striped(idx):
    return np.tile(idx.reshape(-1, 16).T, (8, 1)).astype(np.uint16)


def unstriped(offs):
    return offs[:16].T.reshape(-1).astype(np.int64)


K, T, S, N = 512, 1024, 512, 256
P = 2 ** 7


def setup_inputs():
    n = np.random.standard_normal
    s = mx_kscale(K)[:, None]
    return {
        "xT": (n((K, T)) * s).astype(np.float32),
        "w1": (n((K, N)) / np.sqrt(K) / s).astype(np.float32),
        "prior": np.tile(0.5 * np.random.standard_normal(S), (P, 1)).astype(np.float32),
        "offs": striped(np.random.permutation(T)[:S]),
    }


def reference(xT, w1, prior, offs):
    xq = mxq(f64(xT)[:, unstriped(offs)], 0, "e4m3")
    y = mxq(f64(w1), 0, "e4m3").T @ xq
    yp = y + f64(prior)[:1]
    e = np.exp(yp - yp.max(axis=1, keepdims=True))
    return e / e.sum(axis=1, keepdims=True)

@@ -1,0 +1,86 @@
+from contextlib import ExitStack
+
+import concourse.mybir as mybir
+
+K, T, S, N = 512, 1024, 512, 256
+FLOPS = 2 * K * S * N
+
+F32 = mybir.dt.float32
+BF16 = mybir.dt.bfloat16
+U32 = mybir.dt.uint32
+U16 = mybir.dt.uint16
+U8 = mybir.dt.uint8
+FP8X4 = mybir.dt.float8_e4m3fn_x4
+ALU = mybir.AluOpType
+ACT = mybir.ActivationFunctionType
+
+P = 128
+PACK = 4
+HALF = S // 2
+
+
+def tile_picked_rank_prior_e_kernel(tc, xT, w1, prior, offs, out):
+    nc = tc.nc
+    with ExitStack() as ctx:
+        sb = ctx.enter_context(tc.tile_pool(name="sb", bufs=1))
+        psum = ctx.enter_context(tc.psum_pool(name="psum", bufs=1))
+
+        offsets = sb.tile([P, S // 16], U16, name="offsets")
+        nc.sync.dma_start(offsets[:], offs)
+        x_rows = xT.rearrange("(p j) t -> j p t", j=PACK)
+        planes = [sb.tile([P, T], F32, name="plane%d" % j) for j in range(PACK)]
+        for j in range(PACK):
+            nc.sync.dma_start(planes[j][:], x_rows[j])
+        w_raw = sb.tile([P, PACK, N], F32, name="w_raw")
+        nc.sync.dma_start(w_raw[:], w1.rearrange("(p j) n -> p j n", j=PACK))
+        prior_sb = sb.tile([P, S], F32, name="prior_sb")
+        nc.sync.dma_start(prior_sb[:], prior)
+
+        picked_lo = sb.tile([P, 2, S], BF16, name="picked_lo", align_bytes=64)
+        picked_hi = [sb.tile([P, 2, HALF], BF16, name="picked_hi%d" % h, align_bytes=64) for h in range(2)]
+        woven = [sb.tile([P, HALF, PACK], BF16, name="woven%d" % h, align_bytes=64) for h in range(2)]
+        for j in range(2):
+            nc.vector.tensor_copy(picked_lo[:, j, :], planes[j][:].indirect(offsets[:]))
+        for h in range(2):
+            nc.scalar.copy(woven[h][:, :, 0:2], picked_lo[:, :, h * HALF:(h + 1) * HALF].rearrange("p j s -> p s j"))
+        for j in range(2):
+            for h in range(2):
+                nc.vector.tensor_copy(picked_hi[h][:, j, :], planes[2 + j][:].indirect(offsets[:, h * 16:(h + 1) * 16]))
+        nc.scalar.copy(woven[0][:, :, 2:4], picked_hi[0][:].rearrange("p j s -> p s j"))
+        nc.vector.tensor_copy(woven[1][:, :, 2:4], picked_hi[1][:].rearrange("p j s -> p s j"))
+
+        def quantize(src, width, name):
+            codes = sb.tile([P, width], U32, name=name + "_codes", align_bytes=64)
+            scales = sb.tile([P, width], U8, name=name + "_scales", align_bytes=64)
+            nc.vector.quantize_mx(out=codes[:].bitcast(FP8X4), scales=scales[:], in_=src[:].rearrange("p s j -> p (s j)"))
+            return codes, scales
+
+        w_woven = [sb.tile([P, P, PACK], BF16, name="w_woven%d" % b, align_bytes=64) for b in range(2)]
+        for b in range(2):
+            nc.scalar.copy(w_woven[b][:].rearrange("p (c i) j -> p c j i", i=4),
+                           w_raw[:, :, b * P:(b + 1) * P].rearrange("p j (c i) -> p c j i", i=4))
+        xq, wq = [], []
+        for i in range(2):
+            xq.append(quantize(woven[i], HALF, "x%d" % i))
+            wq.append(quantize(w_woven[i], P, "w%d" % i))
+
+        biased = [sb.tile([P, S], F32, name="biased%d" % b) for b in range(2)]
+        neg_max = [sb.tile([P, 1], F32, name="neg_max%d" % b) for b in range(2)]
+        for b in range(2):
+            for h in range(2):
+                cols = slice(h * HALF, (h + 1) * HALF)
+                acc = psum.tile([P, HALF], F32, name="acc%d%d" % (b, h))
+                nc.tensor.matmul_mx(out=acc[:], lhsT=wq[b][0][:].bitcast(FP8X4), lhsT_scale=wq[b][1][:],
+                                    rhs=xq[h][0][:].bitcast(FP8X4), rhs_scale=xq[h][1][:], start=True, stop=True)
+                nc.vector.tensor_tensor(biased[b][:, cols], acc[:], prior_sb[:, cols], ALU.add)
+        for b in range(2):
+            nc.vector.tensor_reduce(neg_max[b][:], biased[b][:], mybir.AxisListType.X, ALU.max, negate=True)
+        for b in range(2):
+            e = sb.tile([P, S], F32, name="e%d" % b)
+            total = sb.tile([P, 1], F32, name="total%d" % b)
+            nc.scalar.activation(e[:], biased[b][:], ACT.Exp, bias=neg_max[b][:], accum_out=total[:])
+            inv = sb.tile([P, 1], F32, name="inv%d" % b)
+            nc.vector.reciprocal(inv[:], total[:])
+            res = sb.tile([P, S], F32, name="res%d" % b)
+            nc.vector.tensor_scalar(res[:], e[:], inv[:], None, ALU.mult)
+            nc.sync.dma_start(out[b * P:(b + 1) * P, :], res[:])

@@ -17,6 +17,7 @@ ACT = mybir.ActivationFunctionType
 P = 128
 PACK = 4
 HALF = S // 2
+SPLIT = 352
 
 
 def tile_picked_rank_prior_e_kernel(tc, xT, w1, prior, offs, out):
@@ -26,33 +27,34 @@ def tile_picked_rank_prior_e_kernel(tc, xT, w1, prior, offs, out):
         psum = ctx.enter_context(tc.psum_pool(name="psum", bufs=1))
 
         offsets = sb.tile([P, S // 16], U16, name="offsets")
-        nc.sync.dma_start(offsets[:], offs)
-        x_rows = xT.rearrange("(p j) t -> j p t", j=PACK)
-        planes = [sb.tile([P, T], F32, name="plane%d" % j) for j in range(PACK)]
-        for j in range(PACK):
-            nc.sync.dma_start(planes[j][:], x_rows[j])
-        w_raw = sb.tile([P, PACK, N], F32, name="w_raw")
+        x_rows = xT.rearrange("(p u e) t -> u p e t", u=2, e=2)
+        chunks = [[sb.tile([P, 2, T // 2], F32, name="chunk%d%d" % (u, c)) for c in range(2)] for u in range(2)]
+        for u in range(2):
+            for c in range(2):
+                nc.sync.dma_start(chunks[u][c][:], x_rows[u][:, :, c * (T // 2):(c + 1) * (T // 2)])
+                if (u, c) == (0, 0):
+                    nc.sync.dma_start(offsets[:], offs)
+        w_raw = sb.tile([P, PACK, N], F32, name="w_raw", tag="w_raw", align_bytes=64)
         nc.sync.dma_start(w_raw[:], w1.rearrange("(p j) n -> p j n", j=PACK))
         prior_sb = sb.tile([P, S], F32, name="prior_sb")
         nc.sync.dma_start(prior_sb[:], prior)
 
-        picked_lo = sb.tile([P, 2, S], BF16, name="picked_lo", align_bytes=64)
-        picked_hi = [sb.tile([P, 2, HALF], BF16, name="picked_hi%d" % h, align_bytes=64) for h in range(2)]
-        woven = [sb.tile([P, HALF, PACK], BF16, name="woven%d" % h, align_bytes=64) for h in range(2)]
-        for j in range(2):
-            nc.vector.tensor_copy(picked_lo[:, j, :], planes[j][:].indirect(offsets[:]))
-        for h in range(2):
-            nc.scalar.copy(woven[h][:, :, 0:2], picked_lo[:, :, h * HALF:(h + 1) * HALF].rearrange("p j s -> p s j"))
-        for j in range(2):
+        woven = [sb.tile([P, HALF * PACK], BF16, name="woven%d" % h, align_bytes=64) for h in range(2)]
+        for u in range(2):
+            pairs = sb.tile([P, T * 2], BF16, name="pairs%d" % u, align_bytes=64)
+            by_token = pairs[:].rearrange("p (t e) -> p t e", e=2)
+            first, second = [chunks[u][c][:].rearrange("p e t -> p t e") for c in range(2)]
+            nc.scalar.copy(by_token[:, 0:T // 2, :], first)
+            nc.vector.tensor_copy(by_token[:, T // 2:T // 2 + SPLIT, :], second[:, 0:SPLIT, :])
+            nc.scalar.copy(by_token[:, T // 2 + SPLIT:, :], second[:, SPLIT:, :])
             for h in range(2):
-                nc.vector.tensor_copy(picked_hi[h][:, j, :], planes[2 + j][:].indirect(offsets[:, h * 16:(h + 1) * 16]))
-        nc.scalar.copy(woven[0][:, :, 2:4], picked_hi[0][:].rearrange("p j s -> p s j"))
-        nc.vector.tensor_copy(woven[1][:, :, 2:4], picked_hi[1][:].rearrange("p j s -> p s j"))
+                words = woven[h][:].bitcast(U32).rearrange("p (s u) -> p s u", u=2)
+                nc.vector.tensor_copy(words[:, :, u], pairs[:].bitcast(U32).indirect(offsets[:, h * 16:(h + 1) * 16]))
 
-        def quantize(src, width, name):
-            codes = sb.tile([P, width], U32, name=name + "_codes", align_bytes=64)
+        def quantize(src, width, name, tag):
+            codes = sb.tile([P, width], U32, name=name + "_codes", tag=tag, align_bytes=64)
             scales = sb.tile([P, width], U8, name=name + "_scales", align_bytes=64)
-            nc.vector.quantize_mx(out=codes[:].bitcast(FP8X4), scales=scales[:], in_=src[:].rearrange("p s j -> p (s j)"))
+            nc.vector.quantize_mx(out=codes[:].bitcast(FP8X4), scales=scales[:], in_=src)
             return codes, scales
 
         w_woven = [sb.tile([P, P, PACK], BF16, name="w_woven%d" % b, align_bytes=64) for b in range(2)]
@@ -61,8 +63,8 @@ def tile_picked_rank_prior_e_kernel(tc, xT, w1, prior, offs, out):
                            w_raw[:, :, b * P:(b + 1) * P].rearrange("p j (c i) -> p c j i", i=4))
         xq, wq = [], []
         for i in range(2):
-            xq.append(quantize(woven[i], HALF, "x%d" % i))
-            wq.append(quantize(w_woven[i], P, "w%d" % i))
+            xq.append(quantize(woven[i][:], HALF, "x%d" % i, ("x0_codes", "w_raw")[i]))
+            wq.append(quantize(w_woven[i][:].rearrange("p s j -> p (s j)"), P, "w%d" % i, "w%d_codes" % i))
 
         biased = [sb.tile([P, S], F32, name="biased%d" % b) for b in range(2)]
         neg_max = [sb.tile([P, 1], F32, name="neg_max%d" % b) for b in range(2)]

@@ -17,7 +17,7 @@ ACT = mybir.ActivationFunctionType
 P = 128
 PACK = 4
 HALF = S // 2
-SPLIT = 352
+QUARTER = S // 4
 
 
 def tile_picked_rank_prior_e_kernel(tc, xT, w1, prior, offs, out):
@@ -27,29 +27,34 @@ def tile_picked_rank_prior_e_kernel(tc, xT, w1, prior, offs, out):
         psum = ctx.enter_context(tc.psum_pool(name="psum", bufs=1))
 
         offsets = sb.tile([P, S // 16], U16, name="offsets")
-        x_rows = xT.rearrange("(p u e) t -> u p e t", u=2, e=2)
-        chunks = [[sb.tile([P, 2, T // 2], F32, name="chunk%d%d" % (u, c)) for c in range(2)] for u in range(2)]
-        for u in range(2):
-            for c in range(2):
-                nc.sync.dma_start(chunks[u][c][:], x_rows[u][:, :, c * (T // 2):(c + 1) * (T // 2)])
-                if (u, c) == (0, 0):
-                    nc.sync.dma_start(offsets[:], offs)
+        x_rows = xT.rearrange("(p j) t -> j p t", j=PACK)
+        planes = [sb.tile([P, T], F32, name="plane%d" % j) for j in range(PACK)]
+        for j in range(PACK):
+            nc.sync.dma_start(planes[j][:], x_rows[j])
+            if j == 0:
+                nc.sync.dma_start(offsets[:], offs)
         w_raw = sb.tile([P, PACK, N], F32, name="w_raw", tag="w_raw", align_bytes=64)
         nc.sync.dma_start(w_raw[:], w1.rearrange("(p j) n -> p j n", j=PACK))
         prior_sb = sb.tile([P, S], F32, name="prior_sb")
         nc.sync.dma_start(prior_sb[:], prior)
 
+        warm = sb.tile([P, 2], F32, name="warm")
+        nc.gpsimd.memset(warm[:, 0:1], 0.0)
+        nc.scalar.activation(warm[:, 1:2], warm[:, 0:1], ACT.Exp)
+
         woven = [sb.tile([P, HALF * PACK], BF16, name="woven%d" % h, align_bytes=64) for h in range(2)]
         for u in range(2):
-            pairs = sb.tile([P, T * 2], BF16, name="pairs%d" % u, align_bytes=64)
-            by_token = pairs[:].rearrange("p (t e) -> p t e", e=2)
-            first, second = [chunks[u][c][:].rearrange("p e t -> p t e") for c in range(2)]
-            nc.scalar.copy(by_token[:, 0:T // 2, :], first)
-            nc.vector.tensor_copy(by_token[:, T // 2:T // 2 + SPLIT, :], second[:, 0:SPLIT, :])
-            nc.scalar.copy(by_token[:, T // 2 + SPLIT:, :], second[:, SPLIT:, :])
-            for h in range(2):
-                words = woven[h][:].bitcast(U32).rearrange("p (s u) -> p s u", u=2)
-                nc.vector.tensor_copy(words[:, :, u], pairs[:].bitcast(U32).indirect(offsets[:, h * 16:(h + 1) * 16]))
+            quarters = [sb.tile([P, 2, QUARTER], BF16, name="quarter%d%d" % (u, q)) for q in range(2)]
+            second = sb.tile([P, 2, HALF], BF16, name="second%d" % u)
+            for e in range(2):
+                plane = planes[2 * u + e]
+                nc.scalar.activation(second[:, e, :], plane[:].indirect(offsets[:, 16:32]), ACT.Copy)
+                for q in range(2):
+                    nc.vector.tensor_copy(quarters[q][:, e, :], plane[:].indirect(offsets[:, 8 * q:8 * q + 8]))
+            slots = [woven[h][:].rearrange("p (s u e) -> p s u e", u=2, e=2) for h in range(2)]
+            for q in range(2):
+                nc.vector.tensor_copy(slots[0][:, q * QUARTER:(q + 1) * QUARTER, u, :], quarters[q][:].rearrange("p e s -> p s e"))
+            nc.vector.tensor_copy(slots[1][:, :, u, :], second[:].rearrange("p e s -> p s e"))
 
         def quantize(src, width, name, tag):
             codes = sb.tile([P, width], U32, name=name + "_codes", tag=tag, align_bytes=64)
@@ -63,7 +68,7 @@ def tile_picked_rank_prior_e_kernel(tc, xT, w1, prior, offs, out):
                            w_raw[:, :, b * P:(b + 1) * P].rearrange("p j (c i) -> p c j i", i=4))
         xq, wq = [], []
         for i in range(2):
-            xq.append(quantize(woven[i][:], HALF, "x%d" % i, ("x0_codes", "w_raw")[i]))
+            xq.append(quantize(woven[i][:], HALF, "x%d" % i, "x%d_codes" % i))
             wq.append(quantize(w_woven[i][:].rearrange("p s j -> p (s j)"), P, "w%d" % i, "w%d_codes" % i))
 
         biased = [sb.tile([P, S], F32, name="biased%d" % b) for b in range(2)]

@@ -17,7 +17,6 @@ ACT = mybir.ActivationFunctionType
 P = 128
 PACK = 4
 HALF = S // 2
-QUARTER = S // 4
 
 
 def tile_picked_rank_prior_e_kernel(tc, xT, w1, prior, offs, out):
@@ -33,8 +32,10 @@ def tile_picked_rank_prior_e_kernel(tc, xT, w1, prior, offs, out):
             nc.sync.dma_start(planes[j][:], x_rows[j])
             if j == 0:
                 nc.sync.dma_start(offsets[:], offs)
-        w_raw = sb.tile([P, PACK, N], F32, name="w_raw", tag="w_raw", align_bytes=64)
-        nc.sync.dma_start(w_raw[:], w1.rearrange("(p j) n -> p j n", j=PACK))
+        w_rows = w1.rearrange("(p j) n -> p j n", j=PACK)
+        w_raw = [sb.tile([P, PACK, P], F32, name="w_raw%d" % b, tag="w_raw%d" % b, align_bytes=64) for b in range(2)]
+        for b in range(2):
+            nc.sync.dma_start(w_raw[b][:], w_rows[:, :, b * P:(b + 1) * P])
         prior_sb = sb.tile([P, S], F32, name="prior_sb")
         nc.sync.dma_start(prior_sb[:], prior)
 
@@ -43,18 +44,15 @@ def tile_picked_rank_prior_e_kernel(tc, xT, w1, prior, offs, out):
         nc.scalar.activation(warm[:, 1:2], warm[:, 0:1], ACT.Exp)
 
         woven = [sb.tile([P, HALF * PACK], BF16, name="woven%d" % h, align_bytes=64) for h in range(2)]
+        direct = woven[0][:].rearrange("p (s j) -> p s j", j=PACK)
+        slots = woven[1][:].rearrange("p (s u e) -> p s u e", u=2, e=2)
         for u in range(2):
-            quarters = [sb.tile([P, 2, QUARTER], BF16, name="quarter%d%d" % (u, q)) for q in range(2)]
             second = sb.tile([P, 2, HALF], BF16, name="second%d" % u)
             for e in range(2):
-                plane = planes[2 * u + e]
-                nc.scalar.activation(second[:, e, :], plane[:].indirect(offsets[:, 16:32]), ACT.Copy)
-                for q in range(2):
-                    nc.vector.tensor_copy(quarters[q][:, e, :], plane[:].indirect(offsets[:, 8 * q:8 * q + 8]))
-            slots = [woven[h][:].rearrange("p (s u e) -> p s u e", u=2, e=2) for h in range(2)]
-            for q in range(2):
-                nc.vector.tensor_copy(slots[0][:, q * QUARTER:(q + 1) * QUARTER, u, :], quarters[q][:].rearrange("p e s -> p s e"))
-            nc.vector.tensor_copy(slots[1][:, :, u, :], second[:].rearrange("p e s -> p s e"))
+                j = 2 * u + e
+                nc.scalar.activation(second[:, e, :], planes[j][:].indirect(offsets[:, 16:32]), ACT.Copy)
+                nc.vector.tensor_copy(direct[:, :, j], planes[j][:].indirect(offsets[:, 0:16]))
+            nc.vector.tensor_copy(slots[:, :, u, :], second[:].rearrange("p e s -> p s e"))
 
         def quantize(src, width, name, tag):
             codes = sb.tile([P, width], U32, name=name + "_codes", tag=tag, align_bytes=64)
@@ -65,13 +63,13 @@ def tile_picked_rank_prior_e_kernel(tc, xT, w1, prior, offs, out):
         w_woven = [sb.tile([P, P, PACK], BF16, name="w_woven%d" % b, align_bytes=64) for b in range(2)]
         for b in range(2):
             nc.scalar.copy(w_woven[b][:].rearrange("p (c i) j -> p c j i", i=4),
-                           w_raw[:, :, b * P:(b + 1) * P].rearrange("p j (c i) -> p c j i", i=4))
+                           w_raw[b][:].rearrange("p j (c i) -> p c j i", i=4))
         xq, wq = [], []
         for i in range(2):
-            xq.append(quantize(woven[i][:], HALF, "x%d" % i, "x%d_codes" % i))
+            xq.append(quantize(woven[i][:], HALF, "x%d" % i, ("x0_codes", "w_raw0")[i]))
             wq.append(quantize(w_woven[i][:].rearrange("p s j -> p (s j)"), P, "w%d" % i, "w%d_codes" % i))
 
-        biased = [sb.tile([P, S], F32, name="biased%d" % b) for b in range(2)]
+        biased = [sb.tile([P, S], F32, name="biased%d" % b, tag=("w_raw1", "biased1")[b], align_bytes=64) for b in range(2)]
         neg_max = [sb.tile([P, 1], F32, name="neg_max%d" % b) for b in range(2)]
         for b in range(2):
             for h in range(2):

@@ -25,6 +25,8 @@ def tile_picked_rank_prior_e_kernel(tc, xT, w1, prior, offs, out):
         sb = ctx.enter_context(tc.tile_pool(name="sb", bufs=1))
         psum = ctx.enter_context(tc.psum_pool(name="psum", bufs=1))
 
+        prior_cols = sb.tile([P, PACK], F32, name="prior_cols")
+        nc.sync.dma_start(prior_cols[:], prior[0].rearrange("(p t) -> p t", t=PACK))
         offsets = sb.tile([P, S // 16], U16, name="offsets")
         x_rows = xT.rearrange("(p j) t -> j p t", j=PACK)
         planes = [sb.tile([P, T], F32, name="plane%d" % j) for j in range(PACK)]
@@ -36,18 +38,29 @@ def tile_picked_rank_prior_e_kernel(tc, xT, w1, prior, offs, out):
         w_raw = [sb.tile([P, PACK, P], F32, name="w_raw%d" % b, tag="w_raw%d" % b, align_bytes=64) for b in range(2)]
         for b in range(2):
             nc.sync.dma_start(w_raw[b][:], w_rows[:, :, b * P:(b + 1) * P])
-        prior_sb = sb.tile([P, S], F32, name="prior_sb")
-        nc.sync.dma_start(prior_sb[:], prior)
 
-        warm = sb.tile([P, 2], F32, name="warm")
-        nc.gpsimd.memset(warm[:, 0:1], 0.0)
-        nc.scalar.activation(warm[:, 1:2], warm[:, 0:1], ACT.Exp)
+        identity = sb.tile([P, P], F32, name="identity", tag="identity")
+        ones = sb.tile([P, 32], F32, name="ones")
+        nc.vector.memset(ones[:], 1.0)
+        column = sb.tile([P, 32], F32, name="column", align_bytes=64)
+        nc.vector.tensor_tensor_scan(column[:], ones[:], ones[:], 0.0, ALU.mult, ALU.add)
+        row = sb.tile([P, 32], F32, name="row", align_bytes=64)
+        nc.vector.transpose(row[:], column[:])
+        nc.vector.memset(identity[:], 0.0)
+        for q in range(4):
+            part = slice(32 * q, 32 * q + 32)
+            nc.vector.tensor_tensor(identity[part, part], column[part, :], row[part, :], ALU.is_equal)
+        spread = psum.tile([P, PACK, P], F32, name="spread")
+        for t in range(PACK):
+            nc.tensor.transpose(spread[:, t, :], prior_cols[:, t:t + 1].to_broadcast([P, P]), identity[:])
+        prior_sb = sb.tile([P, S], F32, name="prior_sb")
+        nc.scalar.copy(prior_sb[:].rearrange("p (n t) -> p n t", t=PACK), spread[:].rearrange("p t n -> p n t"))
 
         woven = [sb.tile([P, HALF * PACK], BF16, name="woven%d" % h, align_bytes=64) for h in range(2)]
         direct = woven[0][:].rearrange("p (s j) -> p s j", j=PACK)
         slots = woven[1][:].rearrange("p (s u e) -> p s u e", u=2, e=2)
         for u in range(2):
-            second = sb.tile([P, 2, HALF], BF16, name="second%d" % u)
+            second = sb.tile([P, 2, HALF], BF16, name="second%d" % u, tag=("identity", "second1")[u])
             for e in range(2):
                 j = 2 * u + e
                 nc.scalar.activation(second[:, e, :], planes[j][:].indirect(offsets[:, 16:32]), ACT.Copy)

@@ -17,12 +17,14 @@ ACT = mybir.ActivationFunctionType
 P = 128
 PACK = 4
 HALF = S // 2
+W_CUT = 48
 
 
 def tile_picked_rank_prior_e_kernel(tc, xT, w1, prior, offs, out):
     nc = tc.nc
     with ExitStack() as ctx:
         sb = ctx.enter_context(tc.tile_pool(name="sb", bufs=1))
+        shared = ctx.enter_context(tc.tile_pool(name="shared", bufs=1))
         psum = ctx.enter_context(tc.psum_pool(name="psum", bufs=1))
 
         prior_cols = sb.tile([P, PACK], F32, name="prior_cols")
@@ -35,7 +37,8 @@ def tile_picked_rank_prior_e_kernel(tc, xT, w1, prior, offs, out):
             if j == 0:
                 nc.sync.dma_start(offsets[:], offs)
         w_rows = w1.rearrange("(p j) n -> p j n", j=PACK)
-        w_raw = [sb.tile([P, PACK, P], F32, name="w_raw%d" % b, tag="w_raw%d" % b, align_bytes=64) for b in range(2)]
+        w_raw = [shared.tile([P, PACK, P], F32, name="w_raw0", offset=0, align_bytes=64),
+                 sb.tile([P, PACK, P], F32, name="w_raw1", tag="w_raw1", align_bytes=64)]
         for b in range(2):
             nc.sync.dma_start(w_raw[b][:], w_rows[:, :, b * P:(b + 1) * P])
 
@@ -67,20 +70,26 @@ def tile_picked_rank_prior_e_kernel(tc, xT, w1, prior, offs, out):
                 nc.vector.tensor_copy(direct[:, :, j], planes[j][:].indirect(offsets[:, 0:16]))
             nc.vector.tensor_copy(slots[:, :, u, :], second[:].rearrange("p e s -> p s e"))
 
-        def quantize(src, width, name, tag):
-            codes = sb.tile([P, width], U32, name=name + "_codes", tag=tag, align_bytes=64)
-            scales = sb.tile([P, width], U8, name=name + "_scales", align_bytes=64)
+        def quantize(src, codes, name):
+            scales = sb.tile([P, codes.shape[1]], U8, name=name + "_scales", align_bytes=64)
             nc.vector.quantize_mx(out=codes[:].bitcast(FP8X4), scales=scales[:], in_=src)
             return codes, scales
 
-        w_woven = [sb.tile([P, P, PACK], BF16, name="w_woven%d" % b, align_bytes=64) for b in range(2)]
-        for b in range(2):
-            nc.scalar.copy(w_woven[b][:].rearrange("p (c i) j -> p c j i", i=4),
-                           w_raw[b][:].rearrange("p j (c i) -> p c j i", i=4))
-        xq, wq = [], []
-        for i in range(2):
-            xq.append(quantize(woven[i][:], HALF, "x%d" % i, ("x0_codes", "w_raw0")[i]))
-            wq.append(quantize(w_woven[i][:].rearrange("p s j -> p (s j)"), P, "w%d" % i, "w%d_codes" % i))
+        def weave(copy, dst, src, cols):
+            copy(dst[:, cols, :].rearrange("p (c i) j -> p c j i", i=4), src[:, :, cols].rearrange("p j (c i) -> p c j i", i=4))
+
+        w_woven = [sb.tile([P, P, PACK], BF16, name="w_woven0", align_bytes=64),
+                   shared.tile([P, P, PACK], BF16, name="w_woven1", offset=1024, align_bytes=64)]
+        x_codes = [sb.tile([P, HALF], U32, name="x0_codes", align_bytes=64),
+                   shared.tile([P, HALF], U32, name="x1_codes", offset=0, align_bytes=64)]
+        w_codes = [sb.tile([P, P], U32, name="w%d_codes" % b, align_bytes=64) for b in range(2)]
+        weave(nc.scalar.copy, w_woven[0], w_raw[0], slice(0, P))
+        xq = [quantize(woven[0][:], x_codes[0], "x0")]
+        wq = [quantize(w_woven[0][:].rearrange("p s j -> p (s j)"), w_codes[0], "w0")]
+        weave(nc.vector.tensor_copy, w_woven[1], w_raw[1], slice(0, W_CUT))
+        weave(nc.scalar.copy, w_woven[1], w_raw[1], slice(W_CUT, P))
+        xq.append(quantize(woven[1][:], x_codes[1], "x1"))
+        wq.append(quantize(w_woven[1][:].rearrange("p s j -> p (s j)"), w_codes[1], "w1"))
 
         biased = [sb.tile([P, S], F32, name="biased%d" % b, tag=("w_raw1", "biased1")[b], align_bytes=64) for b in range(2)]
         neg_max = [sb.tile([P, 1], F32, name="neg_max%d" % b) for b in range(2)]

@@ -17,6 +17,7 @@ ACT = mybir.ActivationFunctionType
 P = 128
 PACK = 4
 HALF = S // 2
+QUARTER = S // 4
 W_CUT = 48
 
 
@@ -59,15 +60,17 @@ def tile_picked_rank_prior_e_kernel(tc, xT, w1, prior, offs, out):
         prior_sb = sb.tile([P, S], F32, name="prior_sb")
         nc.scalar.copy(prior_sb[:].rearrange("p (n t) -> p n t", t=PACK), spread[:].rearrange("p t n -> p n t"))
 
-        woven = [sb.tile([P, HALF * PACK], BF16, name="woven%d" % h, align_bytes=64) for h in range(2)]
-        direct = woven[0][:].rearrange("p (s j) -> p s j", j=PACK)
-        slots = woven[1][:].rearrange("p (s u e) -> p s u e", u=2, e=2)
+        quarters = [sb.tile([P, QUARTER * PACK], BF16, name="quarter%d" % q, align_bytes=64) for q in range(2)]
+        woven = sb.tile([P, HALF * PACK], BF16, name="woven", align_bytes=64)
+        slots = woven[:].rearrange("p (s u e) -> p s u e", u=2, e=2)
         for u in range(2):
             second = sb.tile([P, 2, HALF], BF16, name="second%d" % u, tag=("identity", "second1")[u])
             for e in range(2):
                 j = 2 * u + e
                 nc.scalar.activation(second[:, e, :], planes[j][:].indirect(offsets[:, 16:32]), ACT.Copy)
-                nc.vector.tensor_copy(direct[:, :, j], planes[j][:].indirect(offsets[:, 0:16]))
+                for q in range(2):
+                    direct = quarters[q][:].rearrange("p (s j) -> p s j", j=PACK)
+                    nc.vector.tensor_copy(direct[:, :, j], planes[j][:].indirect(offsets[:, 8 * q:8 * q + 8]))
             nc.vector.tensor_copy(slots[:, :, u, :], second[:].rearrange("p e s -> p s e"))
 
         def quantize(src, codes, name):
@@ -84,22 +87,27 @@ def tile_picked_rank_prior_e_kernel(tc, xT, w1, prior, offs, out):
                    shared.tile([P, HALF], U32, name="x1_codes", offset=0, align_bytes=64)]
         w_codes = [sb.tile([P, P], U32, name="w%d_codes" % b, align_bytes=64) for b in range(2)]
         weave(nc.scalar.copy, w_woven[0], w_raw[0], slice(0, P))
-        xq = [quantize(woven[0][:], x_codes[0], "x0")]
+        x0_scales = sb.tile([P, HALF], U8, name="x0_scales", align_bytes=64)
+        for q in range(2):
+            cols = slice(q * QUARTER, (q + 1) * QUARTER)
+            nc.vector.quantize_mx(out=x_codes[0][:, cols].bitcast(FP8X4), scales=x0_scales[:, cols], in_=quarters[q][:])
+        xq = [(x_codes[0], x0_scales)]
         wq = [quantize(w_woven[0][:].rearrange("p s j -> p (s j)"), w_codes[0], "w0")]
         weave(nc.vector.tensor_copy, w_woven[1], w_raw[1], slice(0, W_CUT))
         weave(nc.scalar.copy, w_woven[1], w_raw[1], slice(W_CUT, P))
-        xq.append(quantize(woven[1][:], x_codes[1], "x1"))
+        xq.append(quantize(woven[:], x_codes[1], "x1"))
         wq.append(quantize(w_woven[1][:].rearrange("p s j -> p (s j)"), w_codes[1], "w1"))
 
         biased = [sb.tile([P, S], F32, name="biased%d" % b, tag=("w_raw1", "biased1")[b], align_bytes=64) for b in range(2)]
         neg_max = [sb.tile([P, 1], F32, name="neg_max%d" % b) for b in range(2)]
-        for b in range(2):
-            for h in range(2):
-                cols = slice(h * HALF, (h + 1) * HALF)
-                acc = psum.tile([P, HALF], F32, name="acc%d%d" % (b, h))
-                nc.tensor.matmul_mx(out=acc[:], lhsT=wq[b][0][:].bitcast(FP8X4), lhsT_scale=wq[b][1][:],
-                                    rhs=xq[h][0][:].bitcast(FP8X4), rhs_scale=xq[h][1][:], start=True, stop=True)
-                nc.vector.tensor_tensor(biased[b][:, cols], acc[:], prior_sb[:, cols], ALU.add)
+        for b, start, width in ((0, 0, QUARTER), (0, QUARTER, QUARTER), (0, HALF, HALF), (1, 0, HALF), (1, HALF, HALF)):
+            cols = slice(start, start + width)
+            part = slice(start % HALF, start % HALF + width)
+            codes, scales = xq[start // HALF]
+            acc = psum.tile([P, width], F32, name="acc%d_%d" % (b, start))
+            nc.tensor.matmul_mx(out=acc[:], lhsT=wq[b][0][:].bitcast(FP8X4), lhsT_scale=wq[b][1][:],
+                                rhs=codes[:, part].bitcast(FP8X4), rhs_scale=scales[:, part], start=True, stop=True)
+            nc.vector.tensor_tensor(biased[b][:, cols], acc[:], prior_sb[:, cols], ALU.add)
         for b in range(2):
             nc.vector.tensor_reduce(neg_max[b][:], biased[b][:], mybir.AxisListType.X, ALU.max, negate=True)
         for b in range(2):
@@ -108,6 +116,9 @@ def tile_picked_rank_prior_e_kernel(tc, xT, w1, prior, offs, out):
             nc.scalar.activation(e[:], biased[b][:], ACT.Exp, bias=neg_max[b][:], accum_out=total[:])
             inv = sb.tile([P, 1], F32, name="inv%d" % b)
             nc.vector.reciprocal(inv[:], total[:])
-            res = sb.tile([P, S], F32, name="res%d" % b)
-            nc.vector.tensor_scalar(res[:], e[:], inv[:], None, ALU.mult)
-            nc.sync.dma_start(out[b * P:(b + 1) * P, :], res[:])
+            width = (S, HALF)[b]
+            for start in range(0, S, width):
+                cols = slice(start, start + width)
+                res = sb.tile([P, width], F32, name="res%d_%d" % (b, start))
+                nc.vector.tensor_scalar(res[:], e[:, cols], inv[:], None, ALU.mult)
+                nc.sync.dma_start(out[b * P:(b + 1) * P, cols], res[:])

@@ -28,8 +28,6 @@ def tile_picked_rank_prior_e_kernel(tc, xT, w1, prior, offs, out):
         shared = ctx.enter_context(tc.tile_pool(name="shared", bufs=1))
         psum = ctx.enter_context(tc.psum_pool(name="psum", bufs=1))
 
-        prior_cols = sb.tile([P, PACK], F32, name="prior_cols")
-        nc.sync.dma_start(prior_cols[:], prior[0].rearrange("(p t) -> p t", t=PACK))
         offsets = sb.tile([P, S // 16], U16, name="offsets")
         x_rows = xT.rearrange("(p j) t -> j p t", j=PACK)
         planes = [sb.tile([P, T], F32, name="plane%d" % j) for j in range(PACK)]
@@ -43,28 +41,18 @@ def tile_picked_rank_prior_e_kernel(tc, xT, w1, prior, offs, out):
         for b in range(2):
             nc.sync.dma_start(w_raw[b][:], w_rows[:, :, b * P:(b + 1) * P])
 
-        identity = sb.tile([P, P], F32, name="identity", tag="identity")
-        ones = sb.tile([P, 32], F32, name="ones")
-        nc.vector.memset(ones[:], 1.0)
-        column = sb.tile([P, 32], F32, name="column", align_bytes=64)
-        nc.vector.tensor_tensor_scan(column[:], ones[:], ones[:], 0.0, ALU.mult, ALU.add)
-        row = sb.tile([P, 32], F32, name="row", align_bytes=64)
-        nc.vector.transpose(row[:], column[:])
-        nc.vector.memset(identity[:], 0.0)
-        for q in range(4):
-            part = slice(32 * q, 32 * q + 32)
-            nc.vector.tensor_tensor(identity[part, part], column[part, :], row[part, :], ALU.is_equal)
-        spread = psum.tile([P, PACK, P], F32, name="spread")
-        for t in range(PACK):
-            nc.tensor.transpose(spread[:, t, :], prior_cols[:, t:t + 1].to_broadcast([P, P]), identity[:])
         prior_sb = sb.tile([P, S], F32, name="prior_sb")
-        nc.scalar.copy(prior_sb[:].rearrange("p (n t) -> p n t", t=PACK), spread[:].rearrange("p t n -> p n t"))
+        nc.sync.dma_start(prior_sb[:], prior)
+
+        warm = sb.tile([P, 2], F32, name="warm")
+        nc.vector.memset(warm[:, 0:1], 0.0)
+        nc.scalar.activation(warm[:, 1:2], warm[:, 0:1], ACT.Exp)
 
         quarters = [sb.tile([P, QUARTER * PACK], BF16, name="quarter%d" % q, align_bytes=64) for q in range(2)]
         woven = sb.tile([P, HALF * PACK], BF16, name="woven", align_bytes=64)
         slots = woven[:].rearrange("p (s u e) -> p s u e", u=2, e=2)
         for u in range(2):
-            second = sb.tile([P, 2, HALF], BF16, name="second%d" % u, tag=("identity", "second1")[u])
+            second = sb.tile([P, 2, HALF], BF16, name="second%d" % u)
             for e in range(2):
                 j = 2 * u + e
                 nc.scalar.activation(second[:, e, :], planes[j][:].indirect(offsets[:, 16:32]), ACT.Copy)
@@ -120,5 +108,8 @@ def tile_picked_rank_prior_e_kernel(tc, xT, w1, prior, offs, out):
             for start in range(0, S, width):
                 cols = slice(start, start + width)
                 res = sb.tile([P, width], F32, name="res%d_%d" % (b, start))
-                nc.vector.tensor_scalar(res[:], e[:, cols], inv[:], None, ALU.mult)
+                if start == 0:
+                    nc.vector.tensor_scalar(res[:], e[:, cols], inv[:], None, ALU.mult)
+                else:
+                    nc.scalar.activation(res[:], e[:, cols], ACT.Copy, scale=inv[:])
                 nc.sync.dma_start(out[b * P:(b + 1) * P, cols], res[:])

@@ -18,7 +18,6 @@ P = 128
 PACK = 4
 HALF = S // 2
 QUARTER = S // 4
-W_CUT = 48
 
 
 def tile_picked_rank_prior_e_kernel(tc, xT, w1, prior, offs, out):
@@ -69,33 +68,37 @@ def tile_picked_rank_prior_e_kernel(tc, xT, w1, prior, offs, out):
         def weave(copy, dst, src, cols):
             copy(dst[:, cols, :].rearrange("p (c i) j -> p c j i", i=4), src[:, :, cols].rearrange("p j (c i) -> p c j i", i=4))
 
-        w_woven = [sb.tile([P, P, PACK], BF16, name="w_woven0", align_bytes=64),
-                   shared.tile([P, P, PACK], BF16, name="w_woven1", offset=1024, align_bytes=64)]
-        x_codes = [sb.tile([P, HALF], U32, name="x0_codes", align_bytes=64),
-                   shared.tile([P, HALF], U32, name="x1_codes", offset=0, align_bytes=64)]
+        w_woven = [sb.tile([P, P, PACK], BF16, name="w_woven%d" % b, align_bytes=64) for b in range(2)]
         w_codes = [sb.tile([P, P], U32, name="w%d_codes" % b, align_bytes=64) for b in range(2)]
+        first_codes = sb.tile([P, QUARTER], U32, name="first_codes", align_bytes=64)
+        second_codes = shared.tile([P, QUARTER], U32, name="second_codes", offset=1024, align_bytes=64)
+        upper_codes = shared.tile([P, HALF], U32, name="upper_codes", offset=0, align_bytes=64)
+        upper_scales = sb.tile([P, HALF], U8, name="upper_scales", align_bytes=64)
         weave(nc.scalar.copy, w_woven[0], w_raw[0], slice(0, P))
-        x0_scales = sb.tile([P, HALF], U8, name="x0_scales", align_bytes=64)
+        first = quantize(quarters[0][:], first_codes, "first")
+        wq = [quantize(w_woven[0][:].rearrange("p s j -> p (s j)"), w_codes[0], "w0")]
+        second_q = quantize(quarters[1][:], second_codes, "second")
+        weave(nc.scalar.copy, w_woven[1], w_raw[1], slice(0, P))
         for q in range(2):
             cols = slice(q * QUARTER, (q + 1) * QUARTER)
-            nc.vector.quantize_mx(out=x_codes[0][:, cols].bitcast(FP8X4), scales=x0_scales[:, cols], in_=quarters[q][:])
-        xq = [(x_codes[0], x0_scales)]
-        wq = [quantize(w_woven[0][:].rearrange("p s j -> p (s j)"), w_codes[0], "w0")]
-        weave(nc.vector.tensor_copy, w_woven[1], w_raw[1], slice(0, W_CUT))
-        weave(nc.scalar.copy, w_woven[1], w_raw[1], slice(W_CUT, P))
-        xq.append(quantize(woven[:], x_codes[1], "x1"))
+            nc.vector.quantize_mx(out=upper_codes[:, cols].bitcast(FP8X4), scales=upper_scales[:, cols],
+                                  in_=woven[:, q * QUARTER * PACK:(q + 1) * QUARTER * PACK])
         wq.append(quantize(w_woven[1][:].rearrange("p s j -> p (s j)"), w_codes[1], "w1"))
 
         biased = [sb.tile([P, S], F32, name="biased%d" % b, tag=("w_raw1", "biased1")[b], align_bytes=64) for b in range(2)]
         neg_max = [sb.tile([P, 1], F32, name="neg_max%d" % b) for b in range(2)]
-        for b, start, width in ((0, 0, QUARTER), (0, QUARTER, QUARTER), (0, HALF, HALF), (1, 0, HALF), (1, HALF, HALF)):
-            cols = slice(start, start + width)
-            part = slice(start % HALF, start % HALF + width)
-            codes, scales = xq[start // HALF]
-            acc = psum.tile([P, width], F32, name="acc%d_%d" % (b, start))
-            nc.tensor.matmul_mx(out=acc[:], lhsT=wq[b][0][:].bitcast(FP8X4), lhsT_scale=wq[b][1][:],
-                                rhs=codes[:, part].bitcast(FP8X4), rhs_scale=scales[:, part], start=True, stop=True)
-            nc.vector.tensor_tensor(biased[b][:, cols], acc[:], prior_sb[:, cols], ALU.add)
+        lower = [(first[0][:], first[1][:]), (second_q[0][:], second_q[1][:])]
+        upper = [[(upper_codes[:, 0:QUARTER], upper_scales[:, 0:QUARTER]), (upper_codes[:, QUARTER:HALF], upper_scales[:, QUARTER:HALF])],
+                 [(upper_codes[:], upper_scales[:])]]
+        for b in range(2):
+            for h, pieces in enumerate((lower, upper[b])):
+                cols = slice(h * HALF, (h + 1) * HALF)
+                acc = psum.tile([P, HALF], F32, name="acc%d_%d" % (b, h))
+                width = HALF // len(pieces)
+                for n, (codes, scales) in enumerate(pieces):
+                    nc.tensor.matmul_mx(out=acc[:, n * width:(n + 1) * width], lhsT=wq[b][0][:].bitcast(FP8X4), lhsT_scale=wq[b][1][:],
+                                        rhs=codes.bitcast(FP8X4), rhs_scale=scales, start=True, stop=True)
+                nc.vector.tensor_tensor(biased[b][:, cols], acc[:], prior_sb[:, cols], ALU.add)
         for b in range(2):
             nc.vector.tensor_reduce(neg_max[b][:], biased[b][:], mybir.AxisListType.X, ALU.max, negate=True)
         for b in range(2):

@@ -18,6 +18,7 @@ P = 128
 PACK = 4
 HALF = S // 2
 QUARTER = S // 4
+W_CUT = 48
 
 
 def tile_picked_rank_prior_e_kernel(tc, xT, w1, prior, offs, out):
@@ -25,11 +26,13 @@ def tile_picked_rank_prior_e_kernel(tc, xT, w1, prior, offs, out):
     with ExitStack() as ctx:
         sb = ctx.enter_context(tc.tile_pool(name="sb", bufs=1))
         shared = ctx.enter_context(tc.tile_pool(name="shared", bufs=1))
+        last = ctx.enter_context(tc.tile_pool(name="last", bufs=1))
         psum = ctx.enter_context(tc.psum_pool(name="psum", bufs=1))
 
         offsets = sb.tile([P, S // 16], U16, name="offsets")
         x_rows = xT.rearrange("(p j) t -> j p t", j=PACK)
-        planes = [sb.tile([P, T], F32, name="plane%d" % j) for j in range(PACK)]
+        planes = [sb.tile([P, T], F32, name="plane%d" % j) for j in range(PACK - 1)]
+        planes.append(last.tile([P, T], F32, name="plane3", offset=0, align_bytes=64))
         for j in range(PACK):
             nc.sync.dma_start(planes[j][:], x_rows[j])
             if j == 0:
@@ -68,17 +71,19 @@ def tile_picked_rank_prior_e_kernel(tc, xT, w1, prior, offs, out):
         def weave(copy, dst, src, cols):
             copy(dst[:, cols, :].rearrange("p (c i) j -> p c j i", i=4), src[:, :, cols].rearrange("p j (c i) -> p c j i", i=4))
 
-        w_woven = [sb.tile([P, P, PACK], BF16, name="w_woven%d" % b, align_bytes=64) for b in range(2)]
+        w_woven = [sb.tile([P, P, PACK], BF16, name="w_woven0", align_bytes=64),
+                   shared.tile([P, P, PACK], BF16, name="w_woven1", offset=1024, align_bytes=64)]
         w_codes = [sb.tile([P, P], U32, name="w%d_codes" % b, align_bytes=64) for b in range(2)]
         first_codes = sb.tile([P, QUARTER], U32, name="first_codes", align_bytes=64)
-        second_codes = shared.tile([P, QUARTER], U32, name="second_codes", offset=1024, align_bytes=64)
+        second_codes = last.tile([P, QUARTER], U32, name="second_codes", offset=0, align_bytes=64)
         upper_codes = shared.tile([P, HALF], U32, name="upper_codes", offset=0, align_bytes=64)
         upper_scales = sb.tile([P, HALF], U8, name="upper_scales", align_bytes=64)
         weave(nc.scalar.copy, w_woven[0], w_raw[0], slice(0, P))
         first = quantize(quarters[0][:], first_codes, "first")
-        wq = [quantize(w_woven[0][:].rearrange("p s j -> p (s j)"), w_codes[0], "w0")]
         second_q = quantize(quarters[1][:], second_codes, "second")
-        weave(nc.scalar.copy, w_woven[1], w_raw[1], slice(0, P))
+        wq = [quantize(w_woven[0][:].rearrange("p s j -> p (s j)"), w_codes[0], "w0")]
+        weave(nc.vector.tensor_copy, w_woven[1], w_raw[1], slice(0, W_CUT))
+        weave(nc.scalar.copy, w_woven[1], w_raw[1], slice(W_CUT, P))
         for q in range(2):
             cols = slice(q * QUARTER, (q + 1) * QUARTER)
             nc.vector.quantize_mx(out=upper_codes[:, cols].bitcast(FP8X4), scales=upper_scales[:, cols],

@@ -19,6 +19,7 @@ PACK = 4
 HALF = S // 2
 QUARTER = S // 4
 W_CUT = 48
+ROW_ALIGN = 256
 
 
 def tile_picked_rank_prior_e_kernel(tc, xT, w1, prior, offs, out):
@@ -31,19 +32,19 @@ def tile_picked_rank_prior_e_kernel(tc, xT, w1, prior, offs, out):
 
         offsets = sb.tile([P, S // 16], U16, name="offsets")
         x_rows = xT.rearrange("(p j) t -> j p t", j=PACK)
-        planes = [sb.tile([P, T], F32, name="plane%d" % j) for j in range(PACK - 1)]
-        planes.append(last.tile([P, T], F32, name="plane3", offset=0, align_bytes=64))
+        planes = [sb.tile([P, T], F32, name="plane%d" % j, align_bytes=ROW_ALIGN) for j in range(PACK - 1)]
+        planes.append(last.tile([P, T], F32, name="plane3", offset=0, align_bytes=ROW_ALIGN))
         for j in range(PACK):
             nc.sync.dma_start(planes[j][:], x_rows[j])
             if j == 0:
                 nc.sync.dma_start(offsets[:], offs)
         w_rows = w1.rearrange("(p j) n -> p j n", j=PACK)
-        w_raw = [shared.tile([P, PACK, P], F32, name="w_raw0", offset=0, align_bytes=64),
-                 sb.tile([P, PACK, P], F32, name="w_raw1", tag="w_raw1", align_bytes=64)]
+        w_raw = [shared.tile([P, PACK, P], F32, name="w_raw0", offset=0, align_bytes=ROW_ALIGN),
+                 sb.tile([P, PACK, P], F32, name="w_raw1", tag="w_raw1", align_bytes=ROW_ALIGN)]
         for b in range(2):
             nc.sync.dma_start(w_raw[b][:], w_rows[:, :, b * P:(b + 1) * P])
 
-        prior_sb = sb.tile([P, S], F32, name="prior_sb")
+        prior_sb = sb.tile([P, S], F32, name="prior_sb", align_bytes=ROW_ALIGN)
         nc.sync.dma_start(prior_sb[:], prior)
 
         warm = sb.tile([P, 2], F32, name="warm")
@@ -90,7 +91,7 @@ def tile_picked_rank_prior_e_kernel(tc, xT, w1, prior, offs, out):
                                   in_=woven[:, q * QUARTER * PACK:(q + 1) * QUARTER * PACK])
         wq.append(quantize(w_woven[1][:].rearrange("p s j -> p (s j)"), w_codes[1], "w1"))
 
-        biased = [sb.tile([P, S], F32, name="biased%d" % b, tag=("w_raw1", "biased1")[b], align_bytes=64) for b in range(2)]
+        biased = [sb.tile([P, S], F32, name="biased%d" % b, tag=("w_raw1", "biased1")[b], align_bytes=ROW_ALIGN) for b in range(2)]
         neg_max = [sb.tile([P, 1], F32, name="neg_max%d" % b) for b in range(2)]
         lower = [(first[0][:], first[1][:]), (second_q[0][:], second_q[1][:])]
         upper = [[(upper_codes[:, 0:QUARTER], upper_scales[:, 0:QUARTER]), (upper_codes[:, QUARTER:HALF], upper_scales[:, QUARTER:HALF])],
@@ -115,7 +116,7 @@ def tile_picked_rank_prior_e_kernel(tc, xT, w1, prior, offs, out):
             width = (S, HALF)[b]
             for start in range(0, S, width):
                 cols = slice(start, start + width)
-                res = sb.tile([P, width], F32, name="res%d_%d" % (b, start))
+                res = sb.tile([P, width], F32, name="res%d_%d" % (b, start), align_bytes=ROW_ALIGN)
                 if start == 0:
                     nc.vector.tensor_scalar(res[:], e[:, cols], inv[:], None, ALU.mult)
                 else:

@@ -18,7 +18,6 @@ P = 128
 PACK = 4
 HALF = S // 2
 QUARTER = S // 4
-W_CUT = 48
 ROW_ALIGN = 256
 
 
@@ -73,7 +72,7 @@ def tile_picked_rank_prior_e_kernel(tc, xT, w1, prior, offs, out):
             copy(dst[:, cols, :].rearrange("p (c i) j -> p c j i", i=4), src[:, :, cols].rearrange("p j (c i) -> p c j i", i=4))
 
         w_woven = [sb.tile([P, P, PACK], BF16, name="w_woven0", align_bytes=64),
-                   shared.tile([P, P, PACK], BF16, name="w_woven1", offset=1024, align_bytes=64)]
+                   sb.tile([P, P, PACK], BF16, name="w_woven1", align_bytes=64)]
         w_codes = [sb.tile([P, P], U32, name="w%d_codes" % b, align_bytes=64) for b in range(2)]
         first_codes = sb.tile([P, QUARTER], U32, name="first_codes", align_bytes=64)
         second_codes = last.tile([P, QUARTER], U32, name="second_codes", offset=0, align_bytes=64)
@@ -83,8 +82,7 @@ def tile_picked_rank_prior_e_kernel(tc, xT, w1, prior, offs, out):
         first = quantize(quarters[0][:], first_codes, "first")
         second_q = quantize(quarters[1][:], second_codes, "second")
         wq = [quantize(w_woven[0][:].rearrange("p s j -> p (s j)"), w_codes[0], "w0")]
-        weave(nc.vector.tensor_copy, w_woven[1], w_raw[1], slice(0, W_CUT))
-        weave(nc.scalar.copy, w_woven[1], w_raw[1], slice(W_CUT, P))
+        weave(nc.scalar.copy, w_woven[1], w_raw[1], slice(0, P))
         for q in range(2):
             cols = slice(q * QUARTER, (q + 1) * QUARTER)
             nc.vector.quantize_mx(out=upper_codes[:, cols].bitcast(FP8X4), scales=upper_scales[:, cols],

@@ -111,12 +111,7 @@ def tile_picked_rank_prior_e_kernel(tc, xT, w1, prior, offs, out):
             nc.scalar.activation(e[:], biased[b][:], ACT.Exp, bias=neg_max[b][:], accum_out=total[:])
             inv = sb.tile([P, 1], F32, name="inv%d" % b)
             nc.vector.reciprocal(inv[:], total[:])
-            width = (S, HALF)[b]
-            for start in range(0, S, width):
-                cols = slice(start, start + width)
-                res = sb.tile([P, width], F32, name="res%d_%d" % (b, start), align_bytes=ROW_ALIGN)
-                if start == 0:
-                    nc.vector.tensor_scalar(res[:], e[:, cols], inv[:], None, ALU.mult)
-                else:
-                    nc.scalar.activation(res[:], e[:, cols], ACT.Copy, scale=inv[:])
+            for cols in (slice(0, QUARTER), slice(QUARTER, S)):
+                res = sb.tile([P, cols.stop - cols.start], F32, name="res%d_%d" % (b, cols.start), align_bytes=ROW_ALIGN)
+                nc.vector.tensor_scalar(res[:], e[:, cols], inv[:], None, ALU.mult)
                 nc.sync.dma_start(out[b * P:(b + 1) * P, cols], res[:])

@@ -18,7 +18,7 @@ P = 128
 PACK = 4
 HALF = S // 2
 QUARTER = S // 4
-ROW_ALIGN = 256
+ROW_ALIGN = 4096
 
 
 def tile_picked_rank_prior_e_kernel(tc, xT, w1, prior, offs, out):
@@ -26,13 +26,11 @@ def tile_picked_rank_prior_e_kernel(tc, xT, w1, prior, offs, out):
     with ExitStack() as ctx:
         sb = ctx.enter_context(tc.tile_pool(name="sb", bufs=1))
         shared = ctx.enter_context(tc.tile_pool(name="shared", bufs=1))
-        last = ctx.enter_context(tc.tile_pool(name="last", bufs=1))
         psum = ctx.enter_context(tc.psum_pool(name="psum", bufs=1))
 
         offsets = sb.tile([P, S // 16], U16, name="offsets")
         x_rows = xT.rearrange("(p j) t -> j p t", j=PACK)
-        planes = [sb.tile([P, T], F32, name="plane%d" % j, align_bytes=ROW_ALIGN) for j in range(PACK - 1)]
-        planes.append(last.tile([P, T], F32, name="plane3", offset=0, align_bytes=ROW_ALIGN))
+        planes = [sb.tile([P, T], F32, name="plane%d" % j, align_bytes=ROW_ALIGN) for j in range(PACK)]
         for j in range(PACK):
             nc.sync.dma_start(planes[j][:], x_rows[j])
             if j == 0:
@@ -75,13 +73,13 @@ def tile_picked_rank_prior_e_kernel(tc, xT, w1, prior, offs, out):
                    sb.tile([P, P, PACK], BF16, name="w_woven1", align_bytes=64)]
         w_codes = [sb.tile([P, P], U32, name="w%d_codes" % b, align_bytes=64) for b in range(2)]
         first_codes = sb.tile([P, QUARTER], U32, name="first_codes", align_bytes=64)
-        second_codes = last.tile([P, QUARTER], U32, name="second_codes", offset=0, align_bytes=64)
+        second_codes = shared.tile([P, QUARTER], U32, name="second_codes", offset=1024, align_bytes=64)
         upper_codes = shared.tile([P, HALF], U32, name="upper_codes", offset=0, align_bytes=64)
         upper_scales = sb.tile([P, HALF], U8, name="upper_scales", align_bytes=64)
         weave(nc.scalar.copy, w_woven[0], w_raw[0], slice(0, P))
         first = quantize(quarters[0][:], first_codes, "first")
-        second_q = quantize(quarters[1][:], second_codes, "second")
         wq = [quantize(w_woven[0][:].rearrange("p s j -> p (s j)"), w_codes[0], "w0")]
+        second_q = quantize(quarters[1][:], second_codes, "second")
         weave(nc.scalar.copy, w_woven[1], w_raw[1], slice(0, P))
         for q in range(2):
             cols = slice(q * QUARTER, (q + 1) * QUARTER)

@@ -87,26 +87,38 @@ def tile_picked_rank_prior_e_kernel(tc, xT, w1, prior, offs, out):
                                   in_=woven[:, q * QUARTER * PACK:(q + 1) * QUARTER * PACK])
         wq.append(quantize(w_woven[1][:].rearrange("p s j -> p (s j)"), w_codes[1], "w1"))
 
-        biased = [sb.tile([P, S], F32, name="biased%d" % b, tag=("w_raw1", "biased1")[b], align_bytes=ROW_ALIGN) for b in range(2)]
+        biased0 = sb.tile([P, S + 8], F32, name="biased0", tag="w_raw1", align_bytes=ROW_ALIGN)
+        biased1 = sb.tile([P, S], F32, name="biased1", align_bytes=ROW_ALIGN)
+        biased = [biased0, biased1]
         neg_max = [sb.tile([P, 1], F32, name="neg_max%d" % b) for b in range(2)]
-        lower = [(first[0][:], first[1][:]), (second_q[0][:], second_q[1][:])]
-        upper = [[(upper_codes[:, 0:QUARTER], upper_scales[:, 0:QUARTER]), (upper_codes[:, QUARTER:HALF], upper_scales[:, QUARTER:HALF])],
-                 [(upper_codes[:], upper_scales[:])]]
-        for b in range(2):
-            for h, pieces in enumerate((lower, upper[b])):
-                cols = slice(h * HALF, (h + 1) * HALF)
-                acc = psum.tile([P, HALF], F32, name="acc%d_%d" % (b, h))
-                width = HALF // len(pieces)
-                for n, (codes, scales) in enumerate(pieces):
-                    nc.tensor.matmul_mx(out=acc[:, n * width:(n + 1) * width], lhsT=wq[b][0][:].bitcast(FP8X4), lhsT_scale=wq[b][1][:],
-                                        rhs=codes.bitcast(FP8X4), rhs_scale=scales, start=True, stop=True)
-                nc.vector.tensor_tensor(biased[b][:, cols], acc[:], prior_sb[:, cols], ALU.add)
-        for b in range(2):
-            nc.vector.tensor_reduce(neg_max[b][:], biased[b][:], mybir.AxisListType.X, ALU.max, negate=True)
+        pieces = [(first[0][:], first[1][:]), (second_q[0][:], second_q[1][:]),
+                  (upper_codes[:, 0:QUARTER], upper_scales[:, 0:QUARTER]), (upper_codes[:, QUARTER:HALF], upper_scales[:, QUARTER:HALF])]
+
+        def scores(acc, b, codes, scales):
+            nc.tensor.matmul_mx(out=acc, lhsT=wq[b][0][:].bitcast(FP8X4), lhsT_scale=wq[b][1][:],
+                                rhs=codes.bitcast(FP8X4), rhs_scale=scales, start=True, stop=True)
+
+        for h in range(2):
+            acc = psum.tile([P, HALF], F32, name="acc0_%d" % h)
+            for n in range(2):
+                scores(acc[:, n * QUARTER:(n + 1) * QUARTER], 0, *pieces[2 * h + n])
+            nc.vector.tensor_tensor(biased0[:, h * HALF:(h + 1) * HALF], acc[:], prior_sb[:, h * HALF:(h + 1) * HALF], ALU.add)
+        side = psum.tile([P, QUARTER], F32, name="side")
+        scores(side[:], 1, *pieces[0])
+        rest = psum.tile([P, S - QUARTER], F32, name="rest")
+        scores(rest[:, 0:QUARTER], 1, *pieces[1])
+        scores(rest[:, QUARTER:], 1, upper_codes[:], upper_scales[:])
+        side_sb = sb.tile([P, QUARTER], F32, name="side_sb")
+        nc.scalar.copy(side_sb[:], side[:])
+        nc.gpsimd.tensor_tensor(biased1[:, 0:QUARTER], side_sb[:], prior_sb[:, 0:QUARTER], ALU.add)
+        nc.vector.tensor_reduce(biased0[:, S:S + 1], biased0[:, 0:HALF], mybir.AxisListType.X, ALU.max)
+        nc.vector.tensor_tensor(biased1[:, QUARTER:], rest[:], prior_sb[:, QUARTER:], ALU.add)
+        nc.vector.tensor_reduce(neg_max[0][:], biased0[:, HALF:S + 1], mybir.AxisListType.X, ALU.max, negate=True)
+        nc.vector.tensor_reduce(neg_max[1][:], biased1[:], mybir.AxisListType.X, ALU.max, negate=True)
         for b in range(2):
             e = sb.tile([P, S], F32, name="e%d" % b)
             total = sb.tile([P, 1], F32, name="total%d" % b)
-            nc.scalar.activation(e[:], biased[b][:], ACT.Exp, bias=neg_max[b][:], accum_out=total[:])
+            nc.scalar.activation(e[:], biased[b][:, 0:S], ACT.Exp, bias=neg_max[b][:], accum_out=total[:])
             inv = sb.tile([P, 1], F32, name="inv%d" % b)
             nc.vector.reciprocal(inv[:], total[:])
             for cols in (slice(0, QUARTER), slice(QUARTER, S)):

@@ -67,7 +67,7 @@ def tile_picked_rank_prior_e_kernel(tc, xT, w1, prior, offs, out):
             return codes, scales
 
         def weave(copy, dst, src, cols):
-            copy(dst[:, cols, :].rearrange("p (c i) j -> p c j i", i=4), src[:, :, cols].rearrange("p j (c i) -> p c j i", i=4))
+            copy(dst[:, cols, :].rearrange("p (c i) j -> p c j i", i=2), src[:, :, cols].rearrange("p j (c i) -> p c j i", i=2))
 
         w_woven = [sb.tile([P, P, PACK], BF16, name="w_woven0", align_bytes=64),
                    sb.tile([P, P, PACK], BF16, name="w_woven1", align_bytes=64)]

@@ -13,12 +13,18 @@ U8 = mybir.dt.uint8
 FP8X4 = mybir.dt.float8_e4m3fn_x4
 ALU = mybir.AluOpType
 ACT = mybir.ActivationFunctionType
+FREE_AXIS = mybir.AxisListType.X
 
 P = 128
 PACK = 4
+WORD_BYTES = 4
+PER_COLUMN = 16
 HALF = S // 2
 QUARTER = S // 4
+HELPED = 32
 ROW_ALIGN = 4096
+MX_ALIGN = 64
+SPARE = 8
 
 
 def tile_picked_rank_prior_e_kernel(tc, xT, w1, prior, offs, out):
@@ -28,7 +34,7 @@ def tile_picked_rank_prior_e_kernel(tc, xT, w1, prior, offs, out):
         shared = ctx.enter_context(tc.tile_pool(name="shared", bufs=1))
         psum = ctx.enter_context(tc.psum_pool(name="psum", bufs=1))
 
-        offsets = sb.tile([P, S // 16], U16, name="offsets")
+        offsets = sb.tile([P, S // PER_COLUMN], U16, name="offsets")
         x_rows = xT.rearrange("(p j) t -> j p t", j=PACK)
         planes = [sb.tile([P, T], F32, name="plane%d" % j, align_bytes=ROW_ALIGN) for j in range(PACK)]
         for j in range(PACK):
@@ -48,80 +54,88 @@ def tile_picked_rank_prior_e_kernel(tc, xT, w1, prior, offs, out):
         nc.vector.memset(warm[:, 0:1], 0.0)
         nc.scalar.activation(warm[:, 1:2], warm[:, 0:1], ACT.Exp)
 
-        quarters = [sb.tile([P, QUARTER * PACK], BF16, name="quarter%d" % q, align_bytes=64) for q in range(2)]
-        woven = sb.tile([P, HALF * PACK], BF16, name="woven", align_bytes=64)
-        slots = woven[:].rearrange("p (s u e) -> p s u e", u=2, e=2)
+        def entries(start, count):
+            return offsets[:, start // PER_COLUMN:(start + count) // PER_COLUMN]
+
+        lower_in = [sb.tile([P, QUARTER * PACK], BF16, name="quarter%d" % q, align_bytes=MX_ALIGN) for q in range(2)]
+        upper_in = sb.tile([P, HALF * PACK], BF16, name="woven", align_bytes=MX_ALIGN)
+        upper_pairs = upper_in[:].rearrange("p (s u e) -> p s u e", u=2, e=2)
         for u in range(2):
-            second = sb.tile([P, 2, HALF], BF16, name="second%d" % u)
+            runs = sb.tile([P, 2, HALF], BF16, name="second%d" % u)
             for e in range(2):
                 j = 2 * u + e
-                nc.scalar.activation(second[:, e, :], planes[j][:].indirect(offsets[:, 16:32]), ACT.Copy)
+                nc.scalar.activation(runs[:, e, :], planes[j][:].indirect(entries(HALF, HALF)), ACT.Copy)
                 for q in range(2):
-                    direct = quarters[q][:].rearrange("p (s j) -> p s j", j=PACK)
-                    nc.vector.tensor_copy(direct[:, :, j], planes[j][:].indirect(offsets[:, 8 * q:8 * q + 8]))
-            nc.vector.tensor_copy(slots[:, :, u, :], second[:].rearrange("p e s -> p s e"))
+                    by_plane = lower_in[q][:].rearrange("p (s j) -> p s j", j=PACK)
+                    nc.vector.tensor_copy(by_plane[:, :, j], planes[j][:].indirect(entries(q * QUARTER, QUARTER)))
+            nc.vector.tensor_copy(upper_pairs[:, :, u, :], runs[:].rearrange("p e s -> p s e"))
 
         def quantize(src, codes, name):
-            scales = sb.tile([P, codes.shape[1]], U8, name=name + "_scales", align_bytes=64)
+            scales = sb.tile([P, codes.shape[1]], U8, name=name + "_scales", align_bytes=MX_ALIGN)
             nc.vector.quantize_mx(out=codes[:].bitcast(FP8X4), scales=scales[:], in_=src)
-            return codes, scales
+            return codes[:], scales[:]
 
-        def weave(copy, dst, src, cols):
-            copy(dst[:, cols, :].rearrange("p (c i) j -> p c j i", i=2), src[:, :, cols].rearrange("p j (c i) -> p c j i", i=2))
+        def walk(b, cols):
+            return (w_in[b][:, cols, :].rearrange("p (c i) j -> p c j i", i=2), w_raw[b][:, :, cols].rearrange("p j (c i) -> p c j i", i=2))
 
-        w_woven = [sb.tile([P, P, PACK], BF16, name="w_woven0", align_bytes=64),
-                   sb.tile([P, P, PACK], BF16, name="w_woven1", align_bytes=64)]
-        w_codes = [sb.tile([P, P], U32, name="w%d_codes" % b, align_bytes=64) for b in range(2)]
-        first_codes = sb.tile([P, QUARTER], U32, name="first_codes", align_bytes=64)
-        second_codes = shared.tile([P, QUARTER], U32, name="second_codes", offset=1024, align_bytes=64)
-        upper_codes = shared.tile([P, HALF], U32, name="upper_codes", offset=0, align_bytes=64)
-        upper_scales = sb.tile([P, HALF], U8, name="upper_scales", align_bytes=64)
-        weave(nc.scalar.copy, w_woven[0], w_raw[0], slice(0, P))
-        first = quantize(quarters[0][:], first_codes, "first")
-        wq = [quantize(w_woven[0][:].rearrange("p s j -> p (s j)"), w_codes[0], "w0")]
-        second_q = quantize(quarters[1][:], second_codes, "second")
-        weave(nc.scalar.copy, w_woven[1], w_raw[1], slice(0, P))
+        def round_weights(b):
+            nc.scalar.copy(w_in[b][:].rearrange("p (c i) j -> p c j i", i=2), w_raw[b][:].rearrange("p j (c i) -> p c j i", i=2))
+
+        w_in = [sb.tile([P, P, PACK], BF16, name="w_woven%d" % b, align_bytes=MX_ALIGN) for b in range(2)]
+        w_codes = [sb.tile([P, P], U32, name="w%d_codes" % b, align_bytes=MX_ALIGN) for b in range(2)]
+        first_codes = sb.tile([P, QUARTER], U32, name="first_codes", align_bytes=MX_ALIGN)
+        second_codes = shared.tile([P, QUARTER], U32, name="second_codes", offset=HALF * WORD_BYTES, align_bytes=MX_ALIGN)
+        upper_codes = shared.tile([P, HALF], U32, name="upper_codes", offset=0, align_bytes=MX_ALIGN)
+        upper_scales = sb.tile([P, HALF], U8, name="upper_scales", align_bytes=MX_ALIGN)
+        nc.scalar.copy(*walk(0, slice(0, P - HELPED)))
+        nc.gpsimd.tensor_scalar(*walk(0, slice(P - HELPED, P)), 1.0, 0.0, ALU.mult, ALU.add)
+        picked = [quantize(lower_in[0][:], first_codes, "first")]
+        weights = [quantize(w_in[0][:].rearrange("p n j -> p (n j)"), w_codes[0], "w0")]
+        picked.append(quantize(lower_in[1][:], second_codes, "second"))
+        round_weights(1)
         for q in range(2):
             cols = slice(q * QUARTER, (q + 1) * QUARTER)
             nc.vector.quantize_mx(out=upper_codes[:, cols].bitcast(FP8X4), scales=upper_scales[:, cols],
-                                  in_=woven[:, q * QUARTER * PACK:(q + 1) * QUARTER * PACK])
-        wq.append(quantize(w_woven[1][:].rearrange("p s j -> p (s j)"), w_codes[1], "w1"))
+                                  in_=upper_in[:, q * QUARTER * PACK:(q + 1) * QUARTER * PACK])
+            picked.append((upper_codes[:, cols], upper_scales[:, cols]))
+        weights.append(quantize(w_in[1][:].rearrange("p n j -> p (n j)"), w_codes[1], "w1"))
 
-        biased0 = sb.tile([P, S + 8], F32, name="biased0", tag="w_raw1", align_bytes=ROW_ALIGN)
-        biased1 = sb.tile([P, S], F32, name="biased1", align_bytes=ROW_ALIGN)
-        biased = [biased0, biased1]
+        biased = [sb.tile([P, S + SPARE], F32, name="biased0", tag="w_raw1", align_bytes=ROW_ALIGN),
+                  sb.tile([P, S], F32, name="biased1", align_bytes=ROW_ALIGN)]
         neg_max = [sb.tile([P, 1], F32, name="neg_max%d" % b) for b in range(2)]
-        pieces = [(first[0][:], first[1][:]), (second_q[0][:], second_q[1][:]),
-                  (upper_codes[:, 0:QUARTER], upper_scales[:, 0:QUARTER]), (upper_codes[:, QUARTER:HALF], upper_scales[:, QUARTER:HALF])]
 
         def scores(acc, b, codes, scales):
-            nc.tensor.matmul_mx(out=acc, lhsT=wq[b][0][:].bitcast(FP8X4), lhsT_scale=wq[b][1][:],
+            nc.tensor.matmul_mx(out=acc, lhsT=weights[b][0].bitcast(FP8X4), lhsT_scale=weights[b][1],
                                 rhs=codes.bitcast(FP8X4), rhs_scale=scales, start=True, stop=True)
 
         for h in range(2):
+            cols = slice(h * HALF, (h + 1) * HALF)
             acc = psum.tile([P, HALF], F32, name="acc0_%d" % h)
             for n in range(2):
-                scores(acc[:, n * QUARTER:(n + 1) * QUARTER], 0, *pieces[2 * h + n])
-            nc.vector.tensor_tensor(biased0[:, h * HALF:(h + 1) * HALF], acc[:], prior_sb[:, h * HALF:(h + 1) * HALF], ALU.add)
+                scores(acc[:, n * QUARTER:(n + 1) * QUARTER], 0, *picked[2 * h + n])
+            nc.vector.tensor_tensor(biased[0][:, cols], acc[:], prior_sb[:, cols], ALU.add)
+
         side = psum.tile([P, QUARTER], F32, name="side")
-        scores(side[:], 1, *pieces[0])
+        scores(side[:], 1, *picked[0])
         rest = psum.tile([P, S - QUARTER], F32, name="rest")
-        scores(rest[:, 0:QUARTER], 1, *pieces[1])
+        scores(rest[:, 0:QUARTER], 1, *picked[1])
         scores(rest[:, QUARTER:], 1, upper_codes[:], upper_scales[:])
-        side_sb = sb.tile([P, QUARTER], F32, name="side_sb")
+        side_sb = sb.tile([P, QUARTER], F32, name="side_sb", tag="side_sb")
         nc.scalar.copy(side_sb[:], side[:])
-        nc.gpsimd.tensor_tensor(biased1[:, 0:QUARTER], side_sb[:], prior_sb[:, 0:QUARTER], ALU.add)
-        nc.vector.tensor_reduce(biased0[:, S:S + 1], biased0[:, 0:HALF], mybir.AxisListType.X, ALU.max)
-        nc.vector.tensor_tensor(biased1[:, QUARTER:], rest[:], prior_sb[:, QUARTER:], ALU.add)
-        nc.vector.tensor_reduce(neg_max[0][:], biased0[:, HALF:S + 1], mybir.AxisListType.X, ALU.max, negate=True)
-        nc.vector.tensor_reduce(neg_max[1][:], biased1[:], mybir.AxisListType.X, ALU.max, negate=True)
+        nc.gpsimd.tensor_tensor(biased[1][:, 0:QUARTER], side_sb[:], prior_sb[:, 0:QUARTER], ALU.add)
+
+        nc.vector.tensor_reduce(biased[0][:, S:S + 1], biased[0][:, 0:HALF], FREE_AXIS, ALU.max)
+        nc.vector.tensor_tensor(biased[1][:, QUARTER:], rest[:], prior_sb[:, QUARTER:], ALU.add)
+        nc.vector.tensor_reduce(neg_max[0][:], biased[0][:, HALF:S + 1], FREE_AXIS, ALU.max, negate=True)
+        nc.vector.tensor_reduce(neg_max[1][:], biased[1][:], FREE_AXIS, ALU.max, negate=True)
+
         for b in range(2):
-            e = sb.tile([P, S], F32, name="e%d" % b)
+            exps = sb.tile([P, S], F32, name="e%d" % b)
             total = sb.tile([P, 1], F32, name="total%d" % b)
-            nc.scalar.activation(e[:], biased[b][:, 0:S], ACT.Exp, bias=neg_max[b][:], accum_out=total[:])
-            inv = sb.tile([P, 1], F32, name="inv%d" % b)
+            nc.scalar.activation(exps[:], biased[b][:, 0:S], ACT.Exp, bias=neg_max[b][:], accum_out=total[:])
+            inv = sb.tile([P, 1], F32, name="inv%d" % b, tag=("side_sb", "inv1")[b])
             nc.vector.reciprocal(inv[:], total[:])
             for cols in (slice(0, QUARTER), slice(QUARTER, S)):
                 res = sb.tile([P, cols.stop - cols.start], F32, name="res%d_%d" % (b, cols.start), align_bytes=ROW_ALIGN)
-                nc.vector.tensor_scalar(res[:], e[:, cols], inv[:], None, ALU.mult)
+                nc.vector.tensor_scalar(res[:], exps[:, cols], inv[:], None, ALU.mult)
                 nc.sync.dma_start(out[b * P:(b + 1) * P, cols], res[:])

from contextlib import ExitStack

import concourse.mybir as mybir

K, T, S, N = 512, 1024, 512, 256
FLOPS = 2 * K * S * N

F32 = mybir.dt.float32
BF16 = mybir.dt.bfloat16
U32 = mybir.dt.uint32
U16 = mybir.dt.uint16
U8 = mybir.dt.uint8
FP8X4 = mybir.dt.float8_e4m3fn_x4
ALU = mybir.AluOpType
ACT = mybir.ActivationFunctionType
FREE_AXIS = mybir.AxisListType.X

P = 128
PACK = 4
WORD_BYTES = 4
PER_COLUMN = 16
HALF = S // 2
QUARTER = S // 4
HELPED = 32
ROW_ALIGN = 4096
MX_ALIGN = 64
SPARE = 8


def tile_picked_rank_prior_e_kernel(tc, xT, w1, prior, offs, out):
    nc = tc.nc
    with ExitStack() as ctx:
        sb = ctx.enter_context(tc.tile_pool(name="sb", bufs=1))
        shared = ctx.enter_context(tc.tile_pool(name="shared", bufs=1))
        psum = ctx.enter_context(tc.psum_pool(name="psum", bufs=1))

        offsets = sb.tile([P, S // PER_COLUMN], U16, name="offsets")
        x_rows = xT.rearrange("(p j) t -> j p t", j=PACK)
        planes = [sb.tile([P, T], F32, name="plane%d" % j, align_bytes=ROW_ALIGN) for j in range(PACK)]
        for j in range(PACK):
            nc.sync.dma_start(planes[j][:], x_rows[j])
            if j == 0:
                nc.sync.dma_start(offsets[:], offs)
        w_rows = w1.rearrange("(p j) n -> p j n", j=PACK)
        w_raw = [shared.tile([P, PACK, P], F32, name="w_raw0", offset=0, align_bytes=ROW_ALIGN),
                 sb.tile([P, PACK, P], F32, name="w_raw1", tag="w_raw1", align_bytes=ROW_ALIGN)]
        for b in range(2):
            nc.sync.dma_start(w_raw[b][:], w_rows[:, :, b * P:(b + 1) * P])

        prior_sb = sb.tile([P, S], F32, name="prior_sb", align_bytes=ROW_ALIGN)
        nc.sync.dma_start(prior_sb[:], prior)

        warm = sb.tile([P, 2], F32, name="warm")
        nc.vector.memset(warm[:, 0:1], 0.0)
        nc.scalar.activation(warm[:, 1:2], warm[:, 0:1], ACT.Exp)

        def entries(start, count):
            return offsets[:, start // PER_COLUMN:(start + count) // PER_COLUMN]

        lower_in = [sb.tile([P, QUARTER * PACK], BF16, name="quarter%d" % q, align_bytes=MX_ALIGN) for q in range(2)]
        upper_in = sb.tile([P, HALF * PACK], BF16, name="woven", align_bytes=MX_ALIGN)
        upper_pairs = upper_in[:].rearrange("p (s u e) -> p s u e", u=2, e=2)
        for u in range(2):
            runs = sb.tile([P, 2, HALF], BF16, name="second%d" % u)
            for e in range(2):
                j = 2 * u + e
                nc.scalar.activation(runs[:, e, :], planes[j][:].indirect(entries(HALF, HALF)), ACT.Copy)
                for q in range(2):
                    by_plane = lower_in[q][:].rearrange("p (s j) -> p s j", j=PACK)
                    nc.vector.tensor_copy(by_plane[:, :, j], planes[j][:].indirect(entries(q * QUARTER, QUARTER)))
            nc.vector.tensor_copy(upper_pairs[:, :, u, :], runs[:].rearrange("p e s -> p s e"))

        def quantize(src, codes, name):
            scales = sb.tile([P, codes.shape[1]], U8, name=name + "_scales", align_bytes=MX_ALIGN)
            nc.vector.quantize_mx(out=codes[:].bitcast(FP8X4), scales=scales[:], in_=src)
            return codes[:], scales[:]

        def walk(b, cols):
            return (w_in[b][:, cols, :].rearrange("p (c i) j -> p c j i", i=2), w_raw[b][:, :, cols].rearrange("p j (c i) -> p c j i", i=2))

        def round_weights(b):
            nc.scalar.copy(w_in[b][:].rearrange("p (c i) j -> p c j i", i=2), w_raw[b][:].rearrange("p j (c i) -> p c j i", i=2))

        w_in = [sb.tile([P, P, PACK], BF16, name="w_woven%d" % b, align_bytes=MX_ALIGN) for b in range(2)]
        w_codes = [sb.tile([P, P], U32, name="w%d_codes" % b, align_bytes=MX_ALIGN) for b in range(2)]
        first_codes = sb.tile([P, QUARTER], U32, name="first_codes", align_bytes=MX_ALIGN)
        second_codes = shared.tile([P, QUARTER], U32, name="second_codes", offset=HALF * WORD_BYTES, align_bytes=MX_ALIGN)
        upper_codes = shared.tile([P, HALF], U32, name="upper_codes", offset=0, align_bytes=MX_ALIGN)
        upper_scales = sb.tile([P, HALF], U8, name="upper_scales", align_bytes=MX_ALIGN)
        nc.scalar.copy(*walk(0, slice(0, P - HELPED)))
        nc.gpsimd.tensor_scalar(*walk(0, slice(P - HELPED, P)), 1.0, 0.0, ALU.mult, ALU.add)
        picked = [quantize(lower_in[0][:], first_codes, "first")]
        weights = [quantize(w_in[0][:].rearrange("p n j -> p (n j)"), w_codes[0], "w0")]
        picked.append(quantize(lower_in[1][:], second_codes, "second"))
        round_weights(1)
        for q in range(2):
            cols = slice(q * QUARTER, (q + 1) * QUARTER)
            nc.vector.quantize_mx(out=upper_codes[:, cols].bitcast(FP8X4), scales=upper_scales[:, cols],
                                  in_=upper_in[:, q * QUARTER * PACK:(q + 1) * QUARTER * PACK])
            picked.append((upper_codes[:, cols], upper_scales[:, cols]))
        weights.append(quantize(w_in[1][:].rearrange("p n j -> p (n j)"), w_codes[1], "w1"))

        biased = [sb.tile([P, S + SPARE], F32, name="biased0", tag="w_raw1", align_bytes=ROW_ALIGN),
                  sb.tile([P, S], F32, name="biased1", align_bytes=ROW_ALIGN)]
        neg_max = [sb.tile([P, 1], F32, name="neg_max%d" % b) for b in range(2)]

        def scores(acc, b, codes, scales):
            nc.tensor.matmul_mx(out=acc, lhsT=weights[b][0].bitcast(FP8X4), lhsT_scale=weights[b][1],
                                rhs=codes.bitcast(FP8X4), rhs_scale=scales, start=True, stop=True)

        for h in range(2):
            cols = slice(h * HALF, (h + 1) * HALF)
            acc = psum.tile([P, HALF], F32, name="acc0_%d" % h)
            for n in range(2):
                scores(acc[:, n * QUARTER:(n + 1) * QUARTER], 0, *picked[2 * h + n])
            nc.vector.tensor_tensor(biased[0][:, cols], acc[:], prior_sb[:, cols], ALU.add)

        side = psum.tile([P, QUARTER], F32, name="side")
        scores(side[:], 1, *picked[0])
        rest = psum.tile([P, S - QUARTER], F32, name="rest")
        scores(rest[:, 0:QUARTER], 1, *picked[1])
        scores(rest[:, QUARTER:], 1, upper_codes[:], upper_scales[:])
        side_sb = sb.tile([P, QUARTER], F32, name="side_sb", tag="side_sb")
        nc.scalar.copy(side_sb[:], side[:])
        nc.gpsimd.tensor_tensor(biased[1][:, 0:QUARTER], side_sb[:], prior_sb[:, 0:QUARTER], ALU.add)

        nc.vector.tensor_reduce(biased[0][:, S:S + 1], biased[0][:, 0:HALF], FREE_AXIS, ALU.max)
        nc.vector.tensor_tensor(biased[1][:, QUARTER:], rest[:], prior_sb[:, QUARTER:], ALU.add)
        nc.vector.tensor_reduce(neg_max[0][:], biased[0][:, HALF:S + 1], FREE_AXIS, ALU.max, negate=True)
        nc.vector.tensor_reduce(neg_max[1][:], biased[1][:], FREE_AXIS, ALU.max, negate=True)

        for b in range(2):
            exps = sb.tile([P, S], F32, name="e%d" % b)
            total = sb.tile([P, 1], F32, name="total%d" % b)
            nc.scalar.activation(exps[:], biased[b][:, 0:S], ACT.Exp, bias=neg_max[b][:], accum_out=total[:])
            inv = sb.tile([P, 1], F32, name="inv%d" % b, tag=("side_sb", "inv1")[b])
            nc.vector.reciprocal(inv[:], total[:])
            for cols in (slice(0, QUARTER), slice(QUARTER, S)):
                res = sb.tile([P, cols.stop - cols.start], F32, name="res%d_%d" % (b, cols.start), align_bytes=ROW_ALIGN)
                nc.vector.tensor_scalar(res[:], exps[:, cols], inv[:], None, ALU.mult)
                nc.sync.dma_start(out[b * P:(b + 1) * P, cols], res[:])
